import numpy as np
import ml_dtypes


def mxq(x, axis, fmt="e4m3"):
    dtype, down = {"e4m3": (ml_dtypes.float8_e4m3fn, 7), "e5m2": (ml_dtypes.float8_e5m2, 14)}[fmt]
    v = np.moveaxis(np.asarray(x, np.float32).astype(ml_dtypes.bfloat16).astype(np.float64), axis, -1)
    blocks = v.reshape(v.shape[:-1] + (-1, 32))
    amax = np.abs(blocks).max(-1, keepdims=True)
    byte = np.maximum(np.where(amax > 0, np.frexp(amax)[1] - 1 + 127, 0) - down, 1)
    scale = np.exp2(byte - 127.0)
    codes = (blocks / scale).astype(np.float32).astype(dtype).astype(np.float64)
    return np.moveaxis((codes * scale).reshape(v.shape), -1, axis)


WIDE = False


def mx_kscale(k):
    if not WIDE:
        return np.ones(k)
    levels = np.array([10, -10, 5, -5, 0])
    if k % 512:
        return np.exp2(np.random.permutation(np.resize(levels, k // 32))).repeat(32)
    a = np.empty((k // 512, 16))
    for p in range(k // 512):
        a[p, :8] = np.random.permutation(np.resize(levels, 8))
        for g in range(8):
            far = levels[np.abs(levels - a[p, g]) >= 10]
            a[p, g + 8] = far[np.random.randint(len(far))]
    return np.exp2(a.ravel()).repeat(32)


def f64(x):
    return np.asarray(x).astype(np.float64)


def striped(idx):
    return np.tile(idx.reshape(-1, 16).T, (8, 1)).astype(np.uint16)


def unstriped(offs):
    return offs[:16].T.reshape(-1).astype(np.int64)


def pack_weight(w):
    k, n = w.shape
    w = f64(np.asarray(w, np.float32).astype(ml_dtypes.bfloat16)).reshape(k // 32, 32, n)
    amax = np.abs(w).max(1)
    byte = np.clip(np.where(amax > 0, np.frexp(amax)[1] - 1 + 127 - 7, 1), 1, 254)
    scaled = (w * np.exp2(127.0 - byte)[:, None, :]).reshape(k, n).astype(np.float32)
    words = np.ascontiguousarray(scaled.reshape(k // 512, 128, 4, n).transpose(0, 1, 3, 2)).astype(ml_dtypes.float8_e4m3fn).view(np.uint8)
    return words, np.ascontiguousarray(byte.astype(np.uint8).reshape(k // 512, 16, n))


def unpack_weight(words, scales):
    g, p, n, _ = words.shape
    vals = np.ascontiguousarray(words).view(ml_dtypes.float8_e4m3fn).astype(np.float64) * np.repeat(np.exp2(scales.astype(np.float64) - 127.0), 8, axis=1)[..., None]
    return vals.transpose(0, 1, 3, 2).reshape(g * 512, n)


K, T, D, S, V, N = 512, 1024, 8, 4096, 512, 128


def setup_inputs():
    n = np.random.standard_normal
    s = mx_kscale(K)[:, None]
    words, scales = pack_weight(n((K, N)) / np.sqrt(K) / s)
    return {
        "xT": (n((K, T)) * s).astype(np.float32),
        "w_words": words,
        "w_scales": scales,
        "gate": np.tile(np.random.uniform(0.2, 1.0, (D, 1, V)) / np.sqrt(D), (1, N, 1)).astype(np.float32),
        "pos1": striped(np.random.permutation(T)[:V]),
        "pos2": striped(np.random.permutation(T)[:V]),
        "pos3": striped(np.random.permutation(T)[:V]),
        "pos4": striped(np.random.permutation(T)[:V]),
        "pos5": striped(np.random.permutation(T)[:V]),
        "pos6": striped(np.random.permutation(T)[:V]),
        "pos7": striped(np.random.permutation(T)[:V]),
        "pos8": striped(np.random.permutation(T)[:V]),
    }


def reference(xT, w_words, w_scales, gate, pos1, pos2, pos3, pos4, pos5, pos6, pos7, pos8):
    w = unpack_weight(w_words, w_scales)
    y = w.T @ mxq(f64(xT), 0, "e4m3")
    return sum(f64(gate[d]) * y[:, unstriped(p)] for d, p in enumerate((pos1, pos2, pos3, pos4, pos5, pos6, pos7, pos8)))

@@ -1,0 +1,121 @@
+import concourse.mybir as mybir
+
+F32 = mybir.dt.float32
+BF16 = mybir.dt.bfloat16
+U32 = mybir.dt.uint32
+I32 = mybir.dt.int32
+U16 = mybir.dt.uint16
+U8 = mybir.dt.uint8
+FP8X4 = mybir.dt.float8_e4m3fn_x4
+MULT = mybir.AluOpType.mult
+ADD = mybir.AluOpType.add
+
+P = 128
+K, T, D, V, N = 512, 1024, 8, 512, 128
+FLOPS = 2 * K * N * T + 2 * D * N * V
+
+CHUNKS = ((0, 256, 80), (256, 256, 80), (512, 256, 80), (768, 256, 96))
+
+
+def tile_picked_agg_lin_none_sub_l_kernel(
+    tc, xT, w_words, w_scales, gate, pos1, pos2, pos3, pos4, pos5, pos6, pos7, pos8, out
+):
+    nc = tc.nc
+    lists = (pos1, pos2, pos3, pos4, pos5, pos6, pos7, pos8)
+    with (
+        tc.tile_pool(name="held", bufs=1) as held,
+        tc.psum_pool(name="psum", bufs=1) as psum,
+    ):
+        w_codes = held.tile([P, N], U32, align_bytes=64, name="w_codes")
+        w_sc = held.tile([P, N], U8, align_bytes=64, name="w_sc")
+        warm = held.tile([P, 8], F32, name="warm")
+        warm2 = held.tile([P, 8], F32, name="warm2")
+
+        xv = xT.rearrange("(p j) w -> p j w", j=4)
+        raws = []
+        for i, (c0, w, s) in enumerate(CHUNKS):
+            raw = held.tile([P, 4, w], F32, name=f"raw{i}")
+            nc.sync.dma_start(out=raw[:], in_=xv[:, :, c0 : c0 + w])
+            raws.append(raw)
+
+        nc.gpsimd.memset(w_sc[:].bitcast(I32), 0)
+        nc.vector.memset(warm[:], 0.0)
+        nc.scalar.dma_start(
+            out=w_codes[:].bitcast(I32), in_=w_words[0].rearrange("p n t -> p (n t)").bitcast(I32)
+        )
+        for q in range(4):
+            nc.scalar.dma_start(
+                out=w_sc[32 * q : 32 * q + 4, :].bitcast(I32),
+                in_=w_scales[0, 4 * q : 4 * q + 4, :].bitcast(I32),
+            )
+        nc.scalar.copy(out=warm2[:], in_=warm[:])
+
+        offs = []
+        gates = []
+        for d in range(D):
+            off = held.tile([P, V // 16], U16, name=f"off{d}")
+            nc.sync.dma_start(off[:], lists[d])
+            g = held.tile([P, V], F32, name=f"gate{d}")
+            nc.sync.dma_start(out=g[:], in_=gate[d])
+            offs.append(off)
+            gates.append(g)
+
+        y = held.tile([P, T], F32, align_bytes=64, name="y")
+        for i, (c0, w, s) in enumerate(CHUNKS):
+            grouped = held.tile([P, w, 4], BF16, align_bytes=64, name=f"grouped{i}")
+            codes = held.tile([P, w], U32, align_bytes=64, name=f"codes{i}")
+            sc = held.tile([P, w], U8, align_bytes=64, name=f"sc{i}")
+            v = w - s
+            nc.vector.tensor_copy(
+                out=grouped[:, 0:v, :], in_=raws[i][:, :, 0:v].rearrange("p j w -> p w j")
+            )
+            nc.scalar.copy(
+                out=grouped[:, v:w, :], in_=raws[i][:, :, v:w].rearrange("p j w -> p w j")
+            )
+            nc.vector.quantize_mx(
+                out=codes[:].bitcast(FP8X4),
+                scales=sc[:],
+                in_=grouped[:].rearrange("p w j -> p (w j)"),
+            )
+            acc = psum.tile([P, w], F32, name=f"acc{i}")
+            nc.tensor.matmul_mx(
+                out=acc[:],
+                lhsT=w_codes[:].bitcast(FP8X4),
+                lhsT_scale=w_sc[:],
+                rhs=codes[:].bitcast(FP8X4),
+                rhs_scale=sc[:],
+                start=True,
+                stop=True,
+            )
+            nc.scalar.copy(out=y[:, c0 : c0 + w], in_=acc[:])
+
+        prod = held.tile([P, D, V], F32, align_bytes=64, name="prod")
+        s1 = held.tile([P, 2, V], F32, align_bytes=64, name="s1")
+        s2 = held.tile([P, 2, V], F32, align_bytes=64, name="s2")
+        s3 = held.tile([P, V], F32, align_bytes=64, name="s3")
+        s4 = held.tile([P, V], F32, align_bytes=64, name="s4")
+
+        def gather(d):
+            nc.vector.tensor_tensor(prod[:, d, :], y[:].indirect(offs[d][:]), gates[d][:], MULT)
+
+        for d in range(5):
+            gather(d)
+        nc.vector.tensor_tensor(s1[:], prod[:, 0:2, :], prod[:, 2:4, :], ADD)
+        gather(5)
+        gather(6)
+        nc.vector.tensor_tensor(s2[:], s1[:], prod[:, 4:6, :], ADD)
+        H = V // 2
+        nc.vector.tensor_tensor(
+            prod[:, 7, 0:H], y[:].indirect(offs[7][:, 0 : H // 16]), gates[7][:, 0:H], MULT
+        )
+        nc.vector.tensor_tensor(s3[:], s2[:, 0, :], s2[:, 1, :], ADD)
+        nc.vector.tensor_tensor(
+            prod[:, 7, H:V], y[:].indirect(offs[7][:, H // 16 : V // 16]), gates[7][:, H:V], MULT
+        )
+        nc.vector.tensor_tensor(s4[:], s3[:], prod[:, 6, :], ADD)
+        res0 = held.tile([P, H], F32, align_bytes=64, name="res0")
+        res1 = held.tile([P, H], F32, align_bytes=64, name="res1")
+        nc.vector.tensor_tensor(res0[:], s4[:, 0:H], prod[:, 7, 0:H], ADD)
+        nc.sync.dma_start(out=out[:, 0:H], in_=res0[:])
+        nc.vector.tensor_tensor(res1[:], s4[:, H:V], prod[:, 7, H:V], ADD)
+        nc.scalar.dma_start(out=out[:, H:V], in_=res1[:])

@@ -14,7 +14,8 @@ P = 128
 K, T, D, V, N = 512, 1024, 8, 512, 128
 FLOPS = 2 * K * N * T + 2 * D * N * V
 
-CHUNKS = ((0, 256, 80), (256, 256, 80), (512, 256, 80), (768, 256, 96))
+LOADS = ((0, 256), (256, 256), (512, 256), (768, 256))
+CHUNKS = ((0, 0, 256, 0), (1, 256, 256, 0), (2, 512, 256, 0), (3, 768, 128, 0), (3, 896, 128, 48))
 
 
 def tile_picked_agg_lin_none_sub_l_kernel(
@@ -33,21 +34,21 @@ def tile_picked_agg_lin_none_sub_l_kernel(
 
         xv = xT.rearrange("(p j) w -> p j w", j=4)
         raws = []
-        for i, (c0, w, s) in enumerate(CHUNKS):
+        for i, (c0, w) in enumerate(LOADS):
             raw = held.tile([P, 4, w], F32, name=f"raw{i}")
             nc.sync.dma_start(out=raw[:], in_=xv[:, :, c0 : c0 + w])
             raws.append(raw)
+            if i == 0:
+                nc.sync.dma_start(
+                    out=w_codes[:].bitcast(I32), in_=w_words[0].rearrange("p n t -> p (n t)").bitcast(I32)
+                )
+                for q in range(4):
+                    nc.sync.dma_start(
+                        out=w_sc[32 * q : 32 * q + 4, :].bitcast(I32),
+                        in_=w_scales[0, 4 * q : 4 * q + 4, :].bitcast(I32),
+                    )
 
-        nc.gpsimd.memset(w_sc[:].bitcast(I32), 0)
-        nc.vector.memset(warm[:], 0.0)
-        nc.scalar.dma_start(
-            out=w_codes[:].bitcast(I32), in_=w_words[0].rearrange("p n t -> p (n t)").bitcast(I32)
-        )
-        for q in range(4):
-            nc.scalar.dma_start(
-                out=w_sc[32 * q : 32 * q + 4, :].bitcast(I32),
-                in_=w_scales[0, 4 * q : 4 * q + 4, :].bitcast(I32),
-            )
+        nc.gpsimd.memset(warm[:], 0.0)
         nc.scalar.copy(out=warm2[:], in_=warm[:])
 
         offs = []
@@ -61,21 +62,34 @@ def tile_picked_agg_lin_none_sub_l_kernel(
             gates.append(g)
 
         y = held.tile([P, T], F32, align_bytes=64, name="y")
-        for i, (c0, w, s) in enumerate(CHUNKS):
-            grouped = held.tile([P, w, 4], BF16, align_bytes=64, name=f"grouped{i}")
+        grouped = []
+        accs = []
+
+        def interleave(i):
+            r, c0, w, s = CHUNKS[i]
+            raw = raws[r]
+            o = c0 - LOADS[r][0]
+            v = w - s
+            g = held.tile([P, w, 4], BF16, align_bytes=64, name=f"grouped{i}")
+            nc.vector.tensor_copy(
+                out=g[:, 0:v, :].rearrange("p (c i) j -> p c j i", i=4),
+                in_=raw[:, :, o : o + v].rearrange("p j (c i) -> p c j i", i=4),
+            )
+            if s > 0:
+                nc.scalar.copy(
+                    out=g[:, v:w, :].rearrange("p (c i) j -> p c j i", i=4),
+                    in_=raw[:, :, o + v : o + w].rearrange("p j (c i) -> p c j i", i=4),
+                )
+            grouped.append(g)
+
+        def multiply(i):
+            w = CHUNKS[i][2]
             codes = held.tile([P, w], U32, align_bytes=64, name=f"codes{i}")
             sc = held.tile([P, w], U8, align_bytes=64, name=f"sc{i}")
-            v = w - s
-            nc.vector.tensor_copy(
-                out=grouped[:, 0:v, :], in_=raws[i][:, :, 0:v].rearrange("p j w -> p w j")
-            )
-            nc.scalar.copy(
-                out=grouped[:, v:w, :], in_=raws[i][:, :, v:w].rearrange("p j w -> p w j")
-            )
             nc.vector.quantize_mx(
                 out=codes[:].bitcast(FP8X4),
                 scales=sc[:],
-                in_=grouped[:].rearrange("p w j -> p (w j)"),
+                in_=grouped[i][:].rearrange("p w j -> p (w j)"),
             )
             acc = psum.tile([P, w], F32, name=f"acc{i}")
             nc.tensor.matmul_mx(
@@ -87,7 +101,30 @@ def tile_picked_agg_lin_none_sub_l_kernel(
                 start=True,
                 stop=True,
             )
-            nc.scalar.copy(out=y[:, c0 : c0 + w], in_=acc[:])
+            accs.append(acc)
+
+        def bring(i):
+            c0, w = CHUNKS[i][1:3]
+            if i == len(CHUNKS) - 1:
+                nc.vector.tensor_copy(out=y[:, c0 : c0 + w], in_=accs[i][:])
+            else:
+                nc.scalar.copy(out=y[:, c0 : c0 + w], in_=accs[i][:])
+
+        interleave(0)
+        multiply(0)
+        bring(0)
+        interleave(1)
+        multiply(1)
+        bring(1)
+        interleave(2)
+        multiply(2)
+        interleave(3)
+        interleave(4)
+        bring(2)
+        multiply(3)
+        multiply(4)
+        bring(3)
+        bring(4)
 
         prod = held.tile([P, D, V], F32, align_bytes=64, name="prod")
         s1 = held.tile([P, 2, V], F32, align_bytes=64, name="s1")
@@ -104,7 +141,7 @@ def tile_picked_agg_lin_none_sub_l_kernel(
         gather(5)
         gather(6)
         nc.vector.tensor_tensor(s2[:], s1[:], prod[:, 4:6, :], ADD)
-        H = V // 2
+        H = 320
         nc.vector.tensor_tensor(
             prod[:, 7, 0:H], y[:].indirect(offs[7][:, 0 : H // 16]), gates[7][:, 0:H], MULT
         )
@@ -114,8 +151,8 @@ def tile_picked_agg_lin_none_sub_l_kernel(
         )
         nc.vector.tensor_tensor(s4[:], s3[:], prod[:, 6, :], ADD)
         res0 = held.tile([P, H], F32, align_bytes=64, name="res0")
-        res1 = held.tile([P, H], F32, align_bytes=64, name="res1")
+        res1 = held.tile([P, V - H], F32, align_bytes=64, name="res1")
         nc.vector.tensor_tensor(res0[:], s4[:, 0:H], prod[:, 7, 0:H], ADD)
-        nc.sync.dma_start(out=out[:, 0:H], in_=res0[:])
+        nc.scalar.dma_start(out=out[:, 0:H], in_=res0[:])
         nc.vector.tensor_tensor(res1[:], s4[:, H:V], prod[:, 7, H:V], ADD)
-        nc.scalar.dma_start(out=out[:, H:V], in_=res1[:])
+        nc.sync.dma_start(out=out[:, H:V], in_=res1[:])

@@ -1,4 +1,5 @@
 import concourse.mybir as mybir
+from concourse.masks import make_identity
 
 F32 = mybir.dt.float32
 BF16 = mybir.dt.bfloat16
@@ -9,6 +10,7 @@ U8 = mybir.dt.uint8
 FP8X4 = mybir.dt.float8_e4m3fn_x4
 MULT = mybir.AluOpType.mult
 ADD = mybir.AluOpType.add
+COPY = mybir.ActivationFunctionType.Copy
 
 P = 128
 K, T, D, V, N = 512, 1024, 8, 512, 128
@@ -25,7 +27,8 @@ def tile_picked_agg_lin_none_sub_l_kernel(
     lists = (pos1, pos2, pos3, pos4, pos5, pos6, pos7, pos8)
     with (
         tc.tile_pool(name="held", bufs=1) as held,
-        tc.psum_pool(name="psum", bufs=1) as psum,
+        tc.psum_pool(name="psum", bufs=3) as psum,
+        tc.psum_pool(name="ring", bufs=4) as ring,
     ):
         w_codes = held.tile([P, N], U32, align_bytes=64, name="w_codes")
         w_sc = held.tile([P, N], U8, align_bytes=64, name="w_sc")
@@ -51,15 +54,27 @@ def tile_picked_agg_lin_none_sub_l_kernel(
         nc.gpsimd.memset(warm[:], 0.0)
         nc.scalar.copy(out=warm2[:], in_=warm[:])
 
+        ident = held.tile([P, P], F32, name="ident")
+        make_identity(nc, ident[:])
+        rows = held.tile([P, P], F32, name="rows")
+        nc.gpsimd.memset(rows[:], 0.0)
+
         offs = []
-        gates = []
         for d in range(D):
             off = held.tile([P, V // 16], U16, name=f"off{d}")
             nc.sync.dma_start(off[:], lists[d])
-            g = held.tile([P, V], F32, name=f"gate{d}")
-            nc.sync.dma_start(out=g[:], in_=gate[d])
             offs.append(off)
-            gates.append(g)
+            if d == 0:
+                gate0 = held.tile([P, V], F32, name="gate0")
+                nc.sync.dma_start(out=gate0[:], in_=gate[0])
+            if d == 1:
+                for c in range(4):
+                    nc.sync.dma_start(out=rows[8 * c : 8 * c + 8, :], in_=gate[:, 0, 128 * c : 128 * c + 128])
+
+        gt_ps = ring.tile([P, 4, P], F32, name="tp")
+        nc.tensor.transpose(gt_ps[:, 0, :], rows[:], ident[:])
+        gt = held.tile([P, 32], F32, name="gt")
+        nc.scalar.copy(out=gt[:], in_=gt_ps[:, 0, 0:32])
 
         y = held.tile([P, T], F32, align_bytes=64, name="y")
         grouped = []
@@ -91,9 +106,9 @@ def tile_picked_agg_lin_none_sub_l_kernel(
                 scales=sc[:],
                 in_=grouped[i][:].rearrange("p w j -> p (w j)"),
             )
-            acc = psum.tile([P, w], F32, name=f"acc{i}")
+            acc = psum.tile([P, 256], F32, name="acc")
             nc.tensor.matmul_mx(
-                out=acc[:],
+                out=acc[:, 0:w],
                 lhsT=w_codes[:].bitcast(FP8X4),
                 lhsT_scale=w_sc[:],
                 rhs=codes[:].bitcast(FP8X4),
@@ -106,9 +121,9 @@ def tile_picked_agg_lin_none_sub_l_kernel(
         def bring(i):
             c0, w = CHUNKS[i][1:3]
             if i == len(CHUNKS) - 1:
-                nc.vector.tensor_copy(out=y[:, c0 : c0 + w], in_=accs[i][:])
+                nc.vector.tensor_copy(out=y[:, c0 : c0 + w], in_=accs[i][:, 0:w])
             else:
-                nc.scalar.copy(out=y[:, c0 : c0 + w], in_=accs[i][:])
+                nc.scalar.copy(out=y[:, c0 : c0 + w], in_=accs[i][:, 0:w])
 
         interleave(0)
         multiply(0)
@@ -126,33 +141,59 @@ def tile_picked_agg_lin_none_sub_l_kernel(
         bring(3)
         bring(4)
 
-        prod = held.tile([P, D, V], F32, align_bytes=64, name="prod")
-        s1 = held.tile([P, 2, V], F32, align_bytes=64, name="s1")
-        s2 = held.tile([P, 2, V], F32, align_bytes=64, name="s2")
-        s3 = held.tile([P, V], F32, align_bytes=64, name="s3")
-        s4 = held.tile([P, V], F32, align_bytes=64, name="s4")
+        def turn(nb):
+            tp = ring.tile([P, 4, P], F32, name="tp")
+            for c in range(4):
+                nc.tensor.transpose(tp[:, c, :], nb[:, 128 * c : 128 * c + 128], ident[:])
+            return tp
 
-        def gather(d):
-            nc.vector.tensor_tensor(prod[:, d, :], y[:].indirect(offs[d][:]), gates[d][:], MULT)
+        def gt_col(d, c):
+            return gt[:, 8 * c + d : 8 * c + d + 1]
 
-        for d in range(5):
-            gather(d)
-        nc.vector.tensor_tensor(s1[:], prod[:, 0:2, :], prod[:, 2:4, :], ADD)
-        gather(5)
-        gather(6)
-        nc.vector.tensor_tensor(s2[:], s1[:], prod[:, 4:6, :], ADD)
-        H = 320
-        nc.vector.tensor_tensor(
-            prod[:, 7, 0:H], y[:].indirect(offs[7][:, 0 : H // 16]), gates[7][:, 0:H], MULT
-        )
-        nc.vector.tensor_tensor(s3[:], s2[:, 0, :], s2[:, 1, :], ADD)
-        nc.vector.tensor_tensor(
-            prod[:, 7, H:V], y[:].indirect(offs[7][:, H // 16 : V // 16]), gates[7][:, H:V], MULT
-        )
-        nc.vector.tensor_tensor(s4[:], s3[:], prod[:, 6, :], ADD)
-        res0 = held.tile([P, H], F32, align_bytes=64, name="res0")
-        res1 = held.tile([P, V - H], F32, align_bytes=64, name="res1")
-        nc.vector.tensor_tensor(res0[:], s4[:, 0:H], prod[:, 7, 0:H], ADD)
-        nc.scalar.dma_start(out=out[:, 0:H], in_=res0[:])
-        nc.vector.tensor_tensor(res1[:], s4[:, H:V], prod[:, 7, H:V], ADD)
-        nc.sync.dma_start(out=out[:, H:V], in_=res1[:])
+        prod0 = held.tile([P, V], F32, name="prod0")
+        parts = {}
+        total = None
+        for d in range(1, D):
+            nb = held.tile([P, V], F32, name=f"nb{d}")
+            nc.vector.tensor_copy(nb[:], y[:].indirect(offs[d][:]))
+            tp = turn(nb)
+            if d == 2:
+                nc.vector.tensor_tensor(prod0[:], y[:].indirect(offs[0][:]), gate0[:], MULT)
+            if d == 7:
+                break
+            scaled = held.tile([P, 4, P], F32, name=f"scaled{d}")
+            for c in range(4):
+                nc.scalar.activation(out=scaled[:, c, :], in_=tp[:, c, :], func=COPY, scale=gt_col(d, c))
+            parts[d] = scaled
+            if d in (2, 3, 4):
+                new = held.tile([P, 4, P], F32, name=f"sum{d}")
+                nc.gpsimd.tensor_tensor(new[:], (parts[1] if d == 2 else total)[:], scaled[:], ADD)
+                total = new
+        w56 = held.tile([P, 4, P], F32, name="w56")
+        nc.vector.tensor_tensor(w56[:], parts[5][:], parts[6][:], ADD)
+        back4 = ring.tile([P, 4, P], F32, name="tp")
+        for c in range(4):
+            nc.tensor.transpose(back4[:, c, :], total[:, c, :], ident[:])
+        part0 = held.tile([P, V], F32, name="part0")
+        nc.vector.tensor_tensor(part0[:], back4[:].rearrange("p c v -> p (c v)"), prod0[:], ADD)
+        last = held.tile([P, 4, P], F32, name="last")
+        backs = []
+        for c in range(4):
+            nc.vector.scalar_tensor_tensor(
+                out=last[:, c, :], in0=tp[:, c, :], scalar=gt_col(7, c), in1=w56[:, c, :], op0=MULT, op1=ADD
+            )
+        for h in range(2):
+            back = ring.tile([P, 4, P], F32, name="tp")
+            for c in range(2):
+                nc.tensor.transpose(back[:, c, :], last[:, 2 * h + c, :], ident[:])
+            backs.append(back)
+        for h in range(2):
+            res = held.tile([P, 256], F32, name=f"res{h}")
+            nc.vector.tensor_tensor(
+                res[:],
+                backs[h][:, 0:2, :].rearrange("p c v -> p (c v)"),
+                part0[:, 256 * h : 256 * h + 256],
+                ADD,
+            )
+            queue = nc.scalar if h == 0 else nc.sync
+            queue.dma_start(out=out[:, 256 * h : 256 * h + 256], in_=res[:])

@@ -16,8 +16,8 @@ P = 128
 K, T, D, V, N = 512, 1024, 8, 512, 128
 FLOPS = 2 * K * N * T + 2 * D * N * V
 
-LOADS = ((0, 256), (256, 256), (512, 256), (768, 256))
-CHUNKS = ((0, 0, 256, 0), (1, 256, 256, 0), (2, 512, 256, 0), (3, 768, 128, 0), (3, 896, 128, 48))
+LOADS = ((0, 384), (384, 384), (768, 256))
+CHUNKS = ((0, 0, 256, 0), (0, 256, 128, 0), (1, 384, 256, 0), (1, 640, 128, 0), (2, 768, 128, 0), (2, 896, 128, 48))
 
 
 def tile_picked_agg_lin_none_sub_l_kernel(
@@ -126,20 +126,23 @@ def tile_picked_agg_lin_none_sub_l_kernel(
                 nc.scalar.copy(out=y[:, c0 : c0 + w], in_=accs[i][:, 0:w])
 
         interleave(0)
+        interleave(1)
         multiply(0)
         bring(0)
-        interleave(1)
         multiply(1)
         bring(1)
         interleave(2)
-        multiply(2)
         interleave(3)
-        interleave(4)
+        multiply(2)
         bring(2)
         multiply(3)
-        multiply(4)
         bring(3)
+        interleave(4)
+        interleave(5)
+        multiply(4)
+        multiply(5)
         bring(4)
+        bring(5)
 
         def turn(nb):
             tp = ring.tile([P, 4, P], F32, name="tp")
@@ -157,8 +160,6 @@ def tile_picked_agg_lin_none_sub_l_kernel(
             nb = held.tile([P, V], F32, name=f"nb{d}")
             nc.vector.tensor_copy(nb[:], y[:].indirect(offs[d][:]))
             tp = turn(nb)
-            if d == 2:
-                nc.vector.tensor_tensor(prod0[:], y[:].indirect(offs[0][:]), gate0[:], MULT)
             if d == 7:
                 break
             scaled = held.tile([P, 4, P], F32, name=f"scaled{d}")
@@ -169,24 +170,26 @@ def tile_picked_agg_lin_none_sub_l_kernel(
                 new = held.tile([P, 4, P], F32, name=f"sum{d}")
                 nc.gpsimd.tensor_tensor(new[:], (parts[1] if d == 2 else total)[:], scaled[:], ADD)
                 total = new
-        w56 = held.tile([P, 4, P], F32, name="w56")
-        nc.vector.tensor_tensor(w56[:], parts[5][:], parts[6][:], ADD)
+        nc.vector.tensor_tensor(prod0[:], y[:].indirect(offs[0][:]), gate0[:], MULT)
+        near = held.tile([P, 4, P], F32, name="near")
+        for c in range(4):
+            nc.vector.scalar_tensor_tensor(
+                out=near[:, c, :], in0=tp[:, c, :], scalar=gt_col(7, c), in1=parts[5][:, c, :], op0=MULT, op1=ADD
+            )
         back4 = ring.tile([P, 4, P], F32, name="tp")
         for c in range(4):
             nc.tensor.transpose(back4[:, c, :], total[:, c, :], ident[:])
-        part0 = held.tile([P, V], F32, name="part0")
-        nc.vector.tensor_tensor(part0[:], back4[:].rearrange("p c v -> p (c v)"), prod0[:], ADD)
-        last = held.tile([P, 4, P], F32, name="last")
         backs = []
-        for c in range(4):
-            nc.vector.scalar_tensor_tensor(
-                out=last[:, c, :], in0=tp[:, c, :], scalar=gt_col(7, c), in1=w56[:, c, :], op0=MULT, op1=ADD
-            )
         for h in range(2):
+            blocks = slice(2 * h, 2 * h + 2)
+            last = held.tile([P, 2, P], F32, name=f"last{h}")
+            nc.vector.tensor_tensor(last[:], near[:, blocks, :], parts[6][:, blocks, :], ADD)
             back = ring.tile([P, 4, P], F32, name="tp")
             for c in range(2):
-                nc.tensor.transpose(back[:, c, :], last[:, 2 * h + c, :], ident[:])
+                nc.tensor.transpose(back[:, c, :], last[:, c, :], ident[:])
             backs.append(back)
+        part0 = held.tile([P, V], F32, name="part0")
+        nc.vector.tensor_tensor(part0[:], back4[:].rearrange("p c v -> p (c v)"), prod0[:], ADD)
         for h in range(2):
             res = held.tile([P, 256], F32, name=f"res{h}")
             nc.vector.tensor_tensor(

import concourse.mybir as mybir
from concourse.masks import make_identity

F32 = mybir.dt.float32
BF16 = mybir.dt.bfloat16
U32 = mybir.dt.uint32
I32 = mybir.dt.int32
U16 = mybir.dt.uint16
U8 = mybir.dt.uint8
FP8X4 = mybir.dt.float8_e4m3fn_x4
MULT = mybir.AluOpType.mult
ADD = mybir.AluOpType.add
COPY = mybir.ActivationFunctionType.Copy

P = 128
K, T, D, V, N = 512, 1024, 8, 512, 128
FLOPS = 2 * K * N * T + 2 * D * N * V

LOADS = ((0, 384), (384, 384), (768, 256))
CHUNKS = ((0, 0, 256, 0), (0, 256, 128, 0), (1, 384, 256, 0), (1, 640, 128, 0), (2, 768, 128, 0), (2, 896, 128, 48))


def tile_picked_agg_lin_none_sub_l_kernel(
    tc, xT, w_words, w_scales, gate, pos1, pos2, pos3, pos4, pos5, pos6, pos7, pos8, out
):
    nc = tc.nc
    lists = (pos1, pos2, pos3, pos4, pos5, pos6, pos7, pos8)
    with (
        tc.tile_pool(name="held", bufs=1) as held,
        tc.psum_pool(name="psum", bufs=3) as psum,
        tc.psum_pool(name="ring", bufs=4) as ring,
    ):
        w_codes = held.tile([P, N], U32, align_bytes=64, name="w_codes")
        w_sc = held.tile([P, N], U8, align_bytes=64, name="w_sc")
        warm = held.tile([P, 8], F32, name="warm")
        warm2 = held.tile([P, 8], F32, name="warm2")

        xv = xT.rearrange("(p j) w -> p j w", j=4)
        raws = []
        for i, (c0, w) in enumerate(LOADS):
            raw = held.tile([P, 4, w], F32, name=f"raw{i}")
            nc.sync.dma_start(out=raw[:], in_=xv[:, :, c0 : c0 + w])
            raws.append(raw)
            if i == 0:
                nc.sync.dma_start(
                    out=w_codes[:].bitcast(I32), in_=w_words[0].rearrange("p n t -> p (n t)").bitcast(I32)
                )
                for q in range(4):
                    nc.sync.dma_start(
                        out=w_sc[32 * q : 32 * q + 4, :].bitcast(I32),
                        in_=w_scales[0, 4 * q : 4 * q + 4, :].bitcast(I32),
                    )

        nc.gpsimd.memset(warm[:], 0.0)
        nc.scalar.copy(out=warm2[:], in_=warm[:])

        ident = held.tile([P, P], F32, name="ident")
        make_identity(nc, ident[:])
        rows = held.tile([P, P], F32, name="rows")
        nc.gpsimd.memset(rows[:], 0.0)

        offs = []
        for d in range(D):
            off = held.tile([P, V // 16], U16, name=f"off{d}")
            nc.sync.dma_start(off[:], lists[d])
            offs.append(off)
            if d == 0:
                gate0 = held.tile([P, V], F32, name="gate0")
                nc.sync.dma_start(out=gate0[:], in_=gate[0])
            if d == 1:
                for c in range(4):
                    nc.sync.dma_start(out=rows[8 * c : 8 * c + 8, :], in_=gate[:, 0, 128 * c : 128 * c + 128])

        gt_ps = ring.tile([P, 4, P], F32, name="tp")
        nc.tensor.transpose(gt_ps[:, 0, :], rows[:], ident[:])
        gt = held.tile([P, 32], F32, name="gt")
        nc.scalar.copy(out=gt[:], in_=gt_ps[:, 0, 0:32])

        y = held.tile([P, T], F32, align_bytes=64, name="y")
        grouped = []
        accs = []

        def interleave(i):
            r, c0, w, s = CHUNKS[i]
            raw = raws[r]
            o = c0 - LOADS[r][0]
            v = w - s
            g = held.tile([P, w, 4], BF16, align_bytes=64, name=f"grouped{i}")
            nc.vector.tensor_copy(
                out=g[:, 0:v, :].rearrange("p (c i) j -> p c j i", i=4),
                in_=raw[:, :, o : o + v].rearrange("p j (c i) -> p c j i", i=4),
            )
            if s > 0:
                nc.scalar.copy(
                    out=g[:, v:w, :].rearrange("p (c i) j -> p c j i", i=4),
                    in_=raw[:, :, o + v : o + w].rearrange("p j (c i) -> p c j i", i=4),
                )
            grouped.append(g)

        def multiply(i):
            w = CHUNKS[i][2]
            codes = held.tile([P, w], U32, align_bytes=64, name=f"codes{i}")
            sc = held.tile([P, w], U8, align_bytes=64, name=f"sc{i}")
            nc.vector.quantize_mx(
                out=codes[:].bitcast(FP8X4),
                scales=sc[:],
                in_=grouped[i][:].rearrange("p w j -> p (w j)"),
            )
            acc = psum.tile([P, 256], F32, name="acc")
            nc.tensor.matmul_mx(
                out=acc[:, 0:w],
                lhsT=w_codes[:].bitcast(FP8X4),
                lhsT_scale=w_sc[:],
                rhs=codes[:].bitcast(FP8X4),
                rhs_scale=sc[:],
                start=True,
                stop=True,
            )
            accs.append(acc)

        def bring(i):
            c0, w = CHUNKS[i][1:3]
            if i == len(CHUNKS) - 1:
                nc.vector.tensor_copy(out=y[:, c0 : c0 + w], in_=accs[i][:, 0:w])
            else:
                nc.scalar.copy(out=y[:, c0 : c0 + w], in_=accs[i][:, 0:w])

        interleave(0)
        interleave(1)
        multiply(0)
        bring(0)
        multiply(1)
        bring(1)
        interleave(2)
        interleave(3)
        multiply(2)
        bring(2)
        multiply(3)
        bring(3)
        interleave(4)
        interleave(5)
        multiply(4)
        multiply(5)
        bring(4)
        bring(5)

        def turn(nb):
            tp = ring.tile([P, 4, P], F32, name="tp")
            for c in range(4):
                nc.tensor.transpose(tp[:, c, :], nb[:, 128 * c : 128 * c + 128], ident[:])
            return tp

        def gt_col(d, c):
            return gt[:, 8 * c + d : 8 * c + d + 1]

        prod0 = held.tile([P, V], F32, name="prod0")
        parts = {}
        total = None
        for d in range(1, D):
            nb = held.tile([P, V], F32, name=f"nb{d}")
            nc.vector.tensor_copy(nb[:], y[:].indirect(offs[d][:]))
            tp = turn(nb)
            if d == 7:
                break
            scaled = held.tile([P, 4, P], F32, name=f"scaled{d}")
            for c in range(4):
                nc.scalar.activation(out=scaled[:, c, :], in_=tp[:, c, :], func=COPY, scale=gt_col(d, c))
            parts[d] = scaled
            if d in (2, 3, 4):
                new = held.tile([P, 4, P], F32, name=f"sum{d}")
                nc.gpsimd.tensor_tensor(new[:], (parts[1] if d == 2 else total)[:], scaled[:], ADD)
                total = new
        nc.vector.tensor_tensor(prod0[:], y[:].indirect(offs[0][:]), gate0[:], MULT)
        near = held.tile([P, 4, P], F32, name="near")
        for c in range(4):
            nc.vector.scalar_tensor_tensor(
                out=near[:, c, :], in0=tp[:, c, :], scalar=gt_col(7, c), in1=parts[5][:, c, :], op0=MULT, op1=ADD
            )
        back4 = ring.tile([P, 4, P], F32, name="tp")
        for c in range(4):
            nc.tensor.transpose(back4[:, c, :], total[:, c, :], ident[:])
        backs = []
        for h in range(2):
            blocks = slice(2 * h, 2 * h + 2)
            last = held.tile([P, 2, P], F32, name=f"last{h}")
            nc.vector.tensor_tensor(last[:], near[:, blocks, :], parts[6][:, blocks, :], ADD)
            back = ring.tile([P, 4, P], F32, name="tp")
            for c in range(2):
                nc.tensor.transpose(back[:, c, :], last[:, c, :], ident[:])
            backs.append(back)
        part0 = held.tile([P, V], F32, name="part0")
        nc.vector.tensor_tensor(part0[:], back4[:].rearrange("p c v -> p (c v)"), prod0[:], ADD)
        for h in range(2):
            res = held.tile([P, 256], F32, name=f"res{h}")
            nc.vector.tensor_tensor(
                res[:],
                backs[h][:, 0:2, :].rearrange("p c v -> p (c v)"),
                part0[:, 256 * h : 256 * h + 256],
                ADD,
            )
            queue = nc.scalar if h == 0 else nc.sync
            queue.dma_start(out=out[:, 256 * h : 256 * h + 256], in_=res[:])
